import numpy as np, ml_dtypes
CORES = [2,3,42,43,82,83,122,123]
N = 8
import mx_ref
BF = ml_dtypes.bfloat16
def gcols(t, e):
    v = np.concatenate([t.reshape(8, 16, -1, 4), np.zeros((8, 16, 1, 4), BF)], axis=2)
    return np.ascontiguousarray(np.stack([v[g][:, e[g]] for g in range(8)])).reshape(128, -1)
def tile(rs):
    return np.stack(rs, axis=2).reshape(128, -1).astype(BF)
def pick(q, e):
    c = np.concatenate([q[0].reshape(128, -1, 4), np.zeros((128, 1, 4), np.uint8)], axis=1); s = np.concatenate([q[1], np.ones((16, 1), np.uint8)], axis=1)
    return (np.ascontiguousarray(c[:, e].reshape(128, -1)), np.ascontiguousarray(s[:, e]))
def join(*qs):
    return (np.concatenate([q[0] for q in qs], axis=1), np.concatenate([q[1] for q in qs], axis=1))
def put(q, e, v):
    c, s = q[0].reshape(128, -1, 4).copy(), q[1].copy(); c[:, e] = v[0].reshape(128, -1, 4); s[:, e] = v[1]
    return (c.reshape(128, -1), s)
def pk(c, s):
    return (np.ascontiguousarray(c), mx_ref.live(s))
def emit(q):
    return q[0], q[1]
def packed(v, rng):
    q = [mx_ref.quantize(np.ascontiguousarray(v[r])) for r in range(N)]
    return np.stack([a for a, b in q]), np.stack([mx_ref.plane(b, rng) for a, b in q])
def values_of_codes():
    e, c = np.zeros((128, 128, 4), np.float32), np.zeros((128, 2, 4), np.uint8)
    e[np.arange(128), np.arange(128), 0] = 1
    c[:127, :, 0] = np.arange(256).reshape(2, 128).T[:127]
    return mx_ref.matmul(mx_ref.quantize(e.reshape(128, 512).astype(BF)), (c.reshape(128, 8), np.full((16, 2), 127, np.uint8))).T.reshape(-1).astype(np.float64)
CODE_VALUE, SCALE_VALUE = values_of_codes(), 2.0 ** (np.arange(256) - 127.0)
def decode(q):
    return (CODE_VALUE[q[0]].reshape(16, 8, -1, 4) * SCALE_VALUE[q[1]][:, None, :, None] + 0.0).reshape(128, -1).astype(np.float32)
def f(rng, *shape):
    return mx_ref.flush((rng.standard_normal(shape, dtype=np.float32) * np.exp2(rng.integers(-2, 3, shape[:-1] + (1,)))).astype(BF))
def wide(rng, *shape, cols=0):
    v = rng.standard_normal(shape, dtype=np.float32) * np.exp2(rng.integers(-12, 13, shape)).astype(np.float32)
    if cols: v *= np.repeat(np.exp2(rng.integers(-cols, cols + 1, shape[:-2] + (1, shape[-1] // 4))) * (rng.random(shape[:-2] + (1, shape[-1] // 4)) > 0.0625), 4, axis=-1).astype(np.float32)
    return mx_ref.flush(v.astype(BF))
C, R = 512, 2
SETS = np.arange(256)
ONE = (1 << np.arange(8))[:, None]
DECIDE = [16 * g + k for g in range(8) for k in range(10)] + [15]
def bits(b):
    return np.packbits(b, axis=-2, bitorder="little")[..., 0, :].astype(np.int64)
def numbers_of(rng):
    return {"x": np.array(f(rng, N, 128, 4 * C)), "u": np.array(f(rng, N, 128, 512)), "v": np.array(f(rng, N, 128, 512))}
def same(rng, w):
    c, s = packed(np.stack([w] * N), rng)
    return {"wc": c, "ws": np.stack([s[0]] * N)}
def weights(rng, keep=np.ones((8, 16), bool)):
    w = f(rng, 128, 2048).astype(np.float32).reshape(8, 16, 4, 8, 16, 4)
    w = np.where(keep[:, :, None, None, None, None] & keep[:, :, None], w, np.float32(0.0))
    return same(rng, w.reshape(128, 2048).astype(BF))
def setup_inputs(rng):
    return {**numbers_of(rng), **weights(rng)}
def setup_inputs_ties(rng):
    d = numbers_of(rng)
    e = rng.permutation(N)
    x = d["x"].reshape(N, 8, 16, C, 4)
    x[:, :, 0] = rng.integers(0, 3, (N, 8, C, 4)).astype(np.float32).astype(BF)
    x[e[0], 0, 0, :, 3] = 2.0
    x[e[1]] = 0.0
    u = d["u"].reshape(N, 128, 128, 4)
    u[:, :, DECIDE] = 0.0
    for g in range(8):
        u[:, 16 * g, 16 * g, 0] = 1.0
        u[:, 16 * g, 16 * g + 1, 1] = 1.0
        for k in range(8): u[:, 16 * ((g + k) % 8), 16 * g + 2 + k, 2] = 1.0
    u[:, 0, 15, 3] = 1.0
    u[e[2], 0, 15, 3] = -1.0
    keep = np.ones((8, 16), bool)
    keep[:, 0] = False
    return {"x": x.reshape(N, 128, 4 * C), "u": u.reshape(N, 128, 512), "v": d["v"], **weights(rng, keep)}
def setup_inputs_near(rng):
    d = numbers_of(rng)
    x = d["x"].astype(np.float32).reshape(N, 8, 16, C, 4)
    digits = lambda a: ((a[..., None] >> np.arange(4)) & 1) * np.exp2(np.arange(4) - 23.0)
    o = rng.permutation(N)
    n = rng.integers(0, 16, (N, 8, 3, C))
    far = []
    for r in range(N):
        if o[r] % 2 == 0:
            j, g = int(rng.integers(C)), int(rng.integers(5))
            n[r, :, 0, j] = 0
            n[r, g, 0, j] = 15
            n[r, g, 1, j] = 0
            far.append((r, j))
    have = n[:, :, 0] > n[:, :, 1]
    kind = np.where(have[:, 7], np.where(have[:, 6], 2, 1), 0)
    s = digits(2 * (7 - np.count_nonzero(have[:, :7], axis=1)) + rng.integers(0, 2, (N, C)))
    x[:, :, 8:] = 0
    x[:, 5:, :8] = 0
    x[:, :, 8:11] = digits(n)
    x[:, :, 11, :, 0] = 2.0 ** -10
    x[:, 7, 0, :, 0] = 1.0
    for k in range(2):
        x[:, k, 12] = s * (kind == k)[:, :, None]
        x[:, k, 13, :, 0] = (kind == k) * 2.0 ** -10
        x[:, 7 - k, 1, :, 0] = kind == k
    x[:, 5, 1, :, 0] = np.where(kind == 2, -(1.0 + 0.125 * rng.integers(0, 3, (N, C))) * 2.0 ** -30, 0.0)
    for r, j in far: x[r, 7, 1, j, 0] = 2.0 ** 30
    u = d["u"].reshape(N, 128, 128, 4)
    u[:, :, DECIDE] = 0.0
    for r in range(N):
        k = 2.0 ** -30 if o[r] < N // 2 else 1.0
        for g in range(8):
            for i in range(10):
                h = 16 * g + i
                u[r, 112, h, 0] = k
                u[r, 16 * g + 11, h, 0] = k
                u[r, 16 * g + 8 + i if i < 2 else 16 * ((g + i - 2) % 8) + 10, h] = k
    for p, k in ((113, 1.0), (13, 1.0), (97, 2.0 ** -30), (29, 2.0 ** -30), (81, 2.0 ** -30)): u[:, p, 15, 0] = k
    u[:, 12, 15] = 1.0
    u[:, 28, 15] = 2.0 ** -30
    keep = np.zeros((8, 16), bool)
    keep[:5, :8] = True
    return {"x": x.reshape(N, 128, 4 * C).astype(BF), "u": u.reshape(N, 128, 512), "v": d["v"], **weights(rng, keep)}
def setup_inputs_huge(rng):
    d = numbers_of(rng)
    c = rng.integers(0, 2, (N, 1, 1, C, 1)) * 2.0 - 1.0
    x = (0.9 + 0.05 * rng.random((N, 8, 16, C, 4))) * 2.0 ** 30 * c
    u = d["u"].reshape(N, 128, 128, 4)
    u[:, :, DECIDE] = 0.0
    for r in range(N):
        for h in DECIDE[:-1]: u[r, rng.permutation(128)[:64], h] = 2.0 ** 30
        u[r, :, 112] = 0.0
        u[r, :, 15] = (2.0 ** 30 * (1.0 - 0.03 * rng.random((128, 4)))).astype(np.float32).astype(BF)
    w = np.zeros((128, 4, 128, 4), np.float32)
    i = np.arange(128)
    for b in range(4): w[i, b, i, b] = -0.5
    return {"x": x.astype(np.float32).reshape(N, 128, 4 * C).astype(BF), "u": u.reshape(N, 128, 512), "v": d["v"], **same(rng, w.reshape(128, 2048).astype(BF))}
def setup_inputs_few(rng):
    d = numbers_of(rng)
    e = rng.permutation(N)
    x = d["x"].reshape(N, 8, 16, C, 4)
    k = (1.0 + (2 * rng.integers(0, 64, (N, 8, 8, C, 4)) + 1) * 2.0 ** -7) * np.exp2(-rng.integers(8, 15, (N, 8, 8, C, 4)).astype(np.float32))
    x[:, :, 8:] = (k * rng.choice([-1.0, 1.0], (N, 8, 8, C, 4))).astype(np.float32).astype(BF)
    x[:, :, 8, :, 0] = 1.96875
    have = rng.random((N, 8, C)) < 0.5
    have[e[0]] = True
    have[e[1]] = False
    have[e[2]] = np.arange(8)[:, None] == rng.integers(0, 7, C)
    j = int(rng.integers(C))
    have[e[3], 0, j] = False
    have[e[3], 1:, j] = True
    have[:, 7] = False
    x[:, :, 0, :, 0] = np.where(have, 1.0, -1.0).astype(np.float32).astype(BF)
    x[e[3], 0, 2, :, 0] = np.where(have[e[3], 0], -1.0, 1.0).astype(np.float32).astype(BF)
    s = rng.integers(-8, 9, (N, C))
    s[e[0]] = 64 + 8 * rng.integers(0, 8, C)
    s[e[0], C - 1] = 128
    x[:, 0, 1, :, 0] = s.astype(np.float32).astype(BF)
    u = d["u"].reshape(N, 128, 128, 4)
    u[:, :, ::16] = 0.0
    u[:, :, 1::16] = 0.0
    u[:, :, 15] = 0.0
    for h in range(0, 128, 16): u[:, h, h, 0] = 1.0
    u[:, 1, 15, 0] = 1.0
    u[e[3], 112, 112, 0] = 0.0
    u[e[3], 2, 112, 0] = 1.0
    u[e[3], :, 9] = 0.0
    w = f(rng, 128, 2048).astype(np.float32).reshape(8, 16, 4, 8, 16, 4)
    w[:, :, :, :, 8:] = 0
    i = np.arange(8)
    for p in range(8, 16):
        for b in range(4): w[i, p, b, i, p, b] = 32.0
    w[:, 8, 0, :, 8, 0] = 0
    w[:, :, 0, 0, 2] = 0
    w[0, 0, 0, 0, 2, 0] = -64.0
    w[:, :, 0, 7, 0] = 0
    return {"x": x.reshape(N, 128, 4 * C), "u": u.reshape(N, 128, 512), "v": d["v"], **same(rng, w.reshape(128, 2048).astype(BF))}
def setup_inputs_spread(rng):
    d = setup_inputs(rng)
    d["x"] = wide(rng, N, 128, 4 * C, cols=6)
    return d
def check_inputs(d):
    b = []
    for k in ("x", "u", "v"):
        a = np.abs(d[k].astype(np.float32))
        if not (np.isfinite(a).all() and ((a == 0) | (a >= 2.0 ** -30) & (a <= 2.0 ** 30)).all()): b.append("a value of " + k)
    if ((d["wc"] & 0x7F) == 0x7F).any(): b.append("a code of wc that is no number")
    for k in ("wc", "ws"):
        if (d[k] != d[k][:1]).any(): b.append(k + " isn't the same on all ranks")
    none, least, most = [emit(mx_ref.quantize(np.full((128, 16), k, np.float32).astype(BF)))[1][0, 0] for k in (0.0, 2.0 ** -30, 2.0 ** 30)]
    for r in range(N):
        a = mx_ref.live(d["ws"][r])
        if not ((a == none) | (a >= least) & (a <= most)).all(): b.append("a scale of ws")
    return b
def reference(x, u, v, wc, ws):
    qu = [mx_ref.quantize(u[r]) for r in range(N)]
    lay = pk(wc[0], ws[0])
    now = [x[r] for r in range(N)]
    for t in range(R):
        q = [mx_ref.quantize(now[r]) for r in range(N)]
        best, rep = np.zeros((N, 256), np.float32), np.zeros((N, 256), np.int64)
        here, want = np.zeros((N, 8, C), bool), np.zeros((N, 8, C), np.int64)
        for r in range(N):
            s = mx_ref.matmul(qu[r], q[r]) + np.float32(0.0)
            a = s.reshape(8, 16, C)
            here[r] = a[:, 0] > a[:, 1]
            m = bits(here[r])
            want[r] = (m & bits(a[:, 2:10] > a[:, 1:2])) | ONE
            holds = (m & SETS[:, None]) == SETS[:, None]
            strong = np.where(holds, s[15], np.float32(-np.inf))
            rep[r] = np.argmax(strong, axis=1)
            best[r] = np.max(strong, axis=1)
        win = np.argmax(best, axis=0)
        got = pick(join(*q), np.where(np.isfinite(best[win, SETS]), C * win + rep[win, SETS], -1))
        made = tile([mx_ref.matmul(pick(lay, np.arange(128 * b, 128 * b + 128)), got) * np.float32(0.03125) for b in range(4)])
        table = decode(mx_ref.quantize(made)).astype(BF)
        for r in range(N):
            now[r] = (now[r].astype(np.float32) + gcols(table, np.where(here[r], -1, want[r])).astype(np.float32)).astype(BF)
    y, wl = np.zeros((N, 128, C), np.float32), np.zeros((N, 8, C), np.float32)
    oc, osc = np.zeros((N, 128, 4 * C), np.uint8), np.zeros((N, 16, C), np.uint8)
    for r in range(N):
        q = mx_ref.quantize(now[r])
        y[r] = mx_ref.matmul(mx_ref.quantize(v[r]), q)
        wl[r] = want[r]
        oc[r], osc[r] = emit(q)
    return {"y": y, "wl": wl, "oc": oc, "osc": osc}

from concourse.bass import DstId, RemoteDMATransfer
from concourse.mybir import dt, AluOpType, ActivationFunctionType
import comms_topo

A = AluOpType
F = ActivationFunctionType
CODE = "float8_e4m3fn_x4"
NONE = -float(2 ** 84)
LOW = -float(2 ** 85)
MISS = -float(2 ** 90)
ROUNDS = 2
SPOT = [32, 1, 2, 4, 8, 64, 128, 16]

SCRATCH = {}
PLACES = {}


def _sb(name, cols, dtype):
    SCRATCH[name] = ("sbuf", [128, cols], dtype)


def _mx(name, cols):
    _sb(name + "c", cols, CODE)
    _sb(name + "s", cols, "uint8")


def _parts(name, dtype, *parts):
    at = 0
    for n, c in parts:
        PLACES[n] = (name, at)
        at += c
    _sb(name, at, dtype)


for _k in range(8):
    SCRATCH["ps%d" % _k] = ("psum", [128, 512], "float32")
for _n, _c in (("xa", 2048), ("xb", 2048), ("xc", 2048), ("ut", 512), ("vt", 512), ("wm", 512), ("nd", 512), ("zb", 520),
               ("hb", 512), ("zt", 520), ("junk", 1280), ("yt0", 272), ("yt1", 272), ("yt2", 272), ("yt3", 272),
               ("f1", 1032), ("f2", 520), ("f3", 520), ("f4", 520), ("f5", 520), ("f6", 520)):
    _sb(_n, _c, "bfloat16")
for _n, _c in (("sq", 512), ("acc", 16), ("dg", 32), ("yo", 512), ("wo", 512)):
    _sb(_n, _c, "float32")
_parts("work", "float32", ("va", 512), ("vb", 512), ("sa", 520), ("sb", 520), ("ra", 520), ("rb", 520))
_parts("fixed", "float32", ("m8", 8), ("d5", 128), ("d0b", 128), ("lm", 128), ("d3", 32), ("d3b", 32), ("d4", 8), ("im", 256),
       ("yy", 256), ("j64", 8), ("gcol", 8), ("rowm", 8), ("par", 8), ("npar", 8), ("mneg", 8))
_parts("lists", "float32", ("lx", 128), ("ls", 128))
_parts("whole", "int32", ("ip", 128), ("ip2", 128), ("il", 128), ("il2", 128), ("bi", 256), ("bj", 256), ("io1", 8), ("ij1", 8),
       ("ij2", 8), ("ij3", 8), ("ij4", 8), ("ij6", 8))
for _n, _c in (("ulist", 16), ("off", 16), ("offs", 32)):
    _sb(_n, _c, "uint16")
for _n, _c in (("uq", 128), ("up", 256), ("vq", 128), ("wq", 512), ("c1", 1024), ("c2", 512), ("c3", 128), ("c4", 512),
               ("c5", 128), ("c6", 512), ("pq", 128), ("nq", 128), ("zq", 128), ("xq2", 512)):
    _mx(_n, _c)
for _t in range(ROUNDS):
    for _n, _c in (("xq", 640), ("cq", 256), ("lq", 256), ("mq", 64), ("eq", 128), ("tq", 128), ("hq", 128), ("tl", 192)):
        _mx("%s%d" % (_n, _t), _c)
    for _n, _c in (("ss", 4), ("st", 16), ("sx", 4), ("se", 8)):
        _sb("%s%d" % (_n, _t), _c, "float32")
    _parts("choose%d" % _t, "float32", *[("%s%d" % (_n, _t), _c) for _n, _c in (
        ("cc", 8), ("mm", 8), ("pp", 8), ("ch", 4), ("qq", 4), ("ff", 4), ("c2f", 4), ("f2f", 4))])
    _parts("chosen%d" % _t, "uint16", ("om%d" % _t, 8), ("oe%d" % _t, 8))
    for _n in ("offm", "offe"):
        _sb("%s%d" % (_n, _t), 4, "uint16")
SEMAPHORES = ["nv", "ns", "nt", "ng", "lu", "lxa", "lxb", "lw", "lv", "done", "left"] + [
    "%s%d" % (a, t) for t in range(ROUNDS) for a in ("ac", "as", "bc", "bs", "gc", "om", "oe")]


def rank_program(g, core, T, topo):
    rank = T.rank_of(core)
    if rank is None:
        return
    o, block, partner = rank % 4, rank // 4, rank ^ 4
    queue = {"v": g.vector, "s": g.scalar, "t": g.tensor, "g": g, "y": g.sync}
    counter = {"v": "nv", "s": "ns", "t": "nt", "g": "ng"}
    total, known, snaps, seen, waited = {}, {q: {} for q in queue}, {}, {}, {}

    def P(name, a, b, step=1, r0=0, r1=128):
        name, at = PLACES.get(name, (name, 0))
        return (name, at + a, at + b, step, r0, r1)

    def V(p):
        return T[p[0]][:, p[1]:p[2]:p[3]] if p[3] > 1 else T[p[0]][:, p[1]:p[2]]

    def VR(p):
        return T[p[0]][p[4]:p[5], p[1]:p[2]:p[3]] if p[3] > 1 else T[p[0]][p[4]:p[5], p[1]:p[2]]

    def meet(a, b):
        if max(a[4], b[4]) >= min(a[5], b[5]) or max(a[1], b[1]) >= min(a[2], b[2]):
            return False
        return not (a[3] == b[3] and a[3] > 1 and (a[1] - b[1]) % a[3])

    def conflicts(q, reads, writes):
        out = {}
        for p, w in [(p, False) for p in reads] + [(p, True) for p in writes]:
            bank = p[0][:2] == "ps"
            for p2, w2, q2, tok in seen.get(p[0], []):
                if bank:
                    if q2 == q and not (w or w2):
                        continue
                else:
                    if not (w or w2) or not meet(p, p2):
                        continue
                if q2 == q and not w2:
                    continue
                out[tok[0]] = max(out.get(tok[0], 0), tok[1])
        return out

    def wait(q, deps):
        deps = {s: n for s, n in deps.items() if known[q].get(s, 0) < n}
        keep = [s for s in deps if not any(e != s and snaps.get((e, deps[e]), {}).get(s, 0) >= deps[s] for e in deps)]
        for s in keep:
            queue[q].wait_ge(T.sem[s], deps[s])
            waited[s] = max(waited.get(s, 0), deps[s])
            for e, n in [(s, deps[s])] + list(snaps.get((s, deps[s]), {}).items()):
                known[q][e] = max(known[q].get(e, 0), n)

    def note(q, reads, writes, tok):
        for p in reads:
            seen.setdefault(p[0], []).append((p, False, q, tok))
        for p in writes:
            seen.setdefault(p[0], []).append((p, True, q, tok))

    def do(q, call, reads, writes):
        wait(q, conflicts(q, reads, writes))
        s = counter[q]
        total[s] = total.get(s, 0) + 1
        call().then_inc(T.sem[s], 1)
        snaps[(s, total[s])] = dict(known[q])
        note(q, reads, writes, (s, total[s]))

    def dma(q, out, src, s, full, reads, writes):
        wait(q, conflicts("dma", reads, []))
        total[s] = total.get(s, 0) + 16
        queue[q].dma_start(out, src).then_inc(T.sem[s], 16)
        note("dma", reads, writes, (s, full))

    def fill(p, c):
        do("v", lambda: g.vector.memset(VR(p), c), [], [p])

    def tt(out, a, b, op):
        do("v", lambda: g.vector.tensor_tensor(V(out), V(a), V(b), op), [a, b], [out])

    def ts(out, a, s1, op0, s2=None, op1=None, rows=False):
        W = VR if rows else V
        sc = [s for s in (s1, s2) if isinstance(s, tuple)]
        x1, x2 = [V(s) if isinstance(s, tuple) else s for s in (s1, s2)]
        if op1 is None:
            do("v", lambda: g.vector.tensor_scalar(W(out), W(a), x1, None, op0), [a] + sc, [out])
        else:
            do("v", lambda: g.vector.tensor_scalar(W(out), W(a), x1, x2, op0, op1), [a] + sc, [out])

    def copy(out, a):
        do("v", lambda: g.vector.tensor_copy(V(out), V(a)), [a], [out])

    def scan(out, d0, d1, initial, op0, op1):
        do("v", lambda: g.vector.tensor_tensor_scan(V(out), V(d0), V(d1), initial, op0, op1), [d0, d1], [out])

    def act(out, a, func=F.Copy, scale=None):
        if scale is None:
            do("s", lambda: g.scalar.activation(V(out), V(a), func), [a], [out])
        else:
            do("s", lambda: g.scalar.activation(V(out), V(a), func, scale=scale), [a], [out])

    def below(out, r, end, first, step, at):
        src, junk = P(r, first, 512, step), P("junk", at, at + 512 // step)
        do("s", lambda: g.scalar.activation(V(junk), V(src), F.Sign, bias=V(end), scale=-1.0, accum_out=V(out)),
           [src, end], [junk, out])

    def quant(q, a, b, src):
        do("v", lambda: g.vector.quantize_mx(T[q + "c"][:, a:b], T[q + "s"][:, a:b], V(src)), [src],
           [P(q + "c", a, b), P(q + "s", a, b)])

    def mm(bank, n, w, wa, x, xa):
        do("t", lambda: g.tensor.matmul_mx(T["ps%d" % bank][:, 0:n], T[w + "c"][:, wa:wa + 128], T[w + "s"][:, wa:wa + 128],
                                           T[x + "c"][:, xa:xa + n], T[x + "s"][:, xa:xa + n], True, True),
           [P(w + "c", wa, wa + 128), P(w + "s", wa, wa + 128), P(x + "c", xa, xa + n), P(x + "s", xa, xa + n)],
           [P("ps%d" % bank, 0, n)])

    def pick(out, c, d, win, b, lst, e, f):
        i = P(lst, e, f)
        do("v", lambda: g.vector.tensor_copy(T[out + "c"][:, c:d].bitcast(dt.uint32),
                                             T[win + "c"][:, 0:b].bitcast(dt.uint32).indirect(V(i))),
           [P(win + "c", 0, b), i], [P(out + "c", c, d)])
        do("s", lambda: g.scalar.activation(T[out + "s"][:, c:d], T[win + "s"][:, 0:b].indirect(V(i)), F.Copy),
           [P(win + "s", 0, b), i], [P(out + "s", c, d)])

    def ps(k, a, b, r1=128):
        return P("ps%d" % k, a, b, 1, 0, r1)

    def address(r):
        rid, pid = topo.addr(T.cores[r])[:2]
        return DstId(rid=rid, pnc=pid)

    def bitmask(engines):
        return sum(1 << e for e in engines)

    mates = [4 * block + d for d in range(4) if d != o]
    far = [r for r in mates if topo.chip(T.cores[r]) != topo.chip(core)]
    near = [r for r in mates if r not in far]
    outside = topo.engines(core, T.cores[far[0]])
    share = len(outside) // len(far)
    masks = {r: bitmask(outside[k * share:(k + 1) * share]) for k, r in enumerate(far)}
    inside = [e for e in topo.engines(core, T.cores[near[0]]) if e not in outside]
    for k, r in enumerate(near):
        masks[r] = bitmask(inside[k * share:(k + 1) * share])
    masks[partner] = topo.mask(core, T.cores[partner])

    def send(moves, s, reads):
        wait("g", conflicts("g", reads, []))
        g.remote_dma_fused([RemoteDMATransfer(dst_ids=[address(r)], dma_engine_mask=masks[r], remote_sem=T.sem[s], src=a, dst=b)
                            for r, a, b in moves], local_sem=T.sem.left)
        total["left"] = total.get("left", 0) + sum(bin(masks[r]).count("1") for r, a, b in moves)

    def land(s, n, places):
        total[s] = n
        note("remote", [], places, (s, n))

    def U8(name, a, b):
        return T[name][:, a:b].bitcast(dt.uint8)

    dma("y", T.ut[:], T.u[:], "lu", 16, [], [P("ut", 0, 512)])
    dma("s", T.xa[:, 0:1024], T.x[:, 0:1024], "lxa", 16, [], [P("xa", 0, 1024)])
    dma("y", T.xa[:, 1024:2048], T.x[:, 1024:2048], "lxb", 16, [], [P("xa", 1024, 2048)])
    dma("y", U8("wqc", 0, 512), T.wc[:], "lw", 32, [], [P("wqc", 0, 512)])
    dma("y", T.wqs[:], T.ws[:], "lw", 32, [], [P("wqs", 0, 512)])
    dma("y", T.vt[:], T.v[:], "lv", 16, [], [P("vt", 0, 512)])

    def iota(p, pattern, base, ch, f=False):
        if f:
            do("g", lambda: g.iota(V(p), pattern, base, ch, allow_small_or_imprecise_dtypes=True), [], [p])
        else:
            do("g", lambda: g.iota(V(p), pattern, base, ch), [], [p])

    def select(out, src, pattern, op, value, base, ch):
        do("g", lambda: g.affine_select(V(out), V(src), pattern, op, value, base, ch), [src], [out])

    iota(P("io1", 0, 8), [[16, 8]], 1, 0)
    iota(P("ij2", 0, 8), [[0, 8]], 0, 1)
    iota(P("im", 0, 256), [[1, 256]], 0, 0, True)
    iota(P("ip", 0, 128), [[-2, 128]], 256, 1)
    fill(P("zt", 0, 520), 0.0)
    act(P("f1", 0, 516), P("zt", 0, 516))
    act(P("f1", 516, 1032), P("zt", 0, 516))
    for f in ("f5", "f2", "zb"):
        act(P(f, 0, 520), P("zt", 0, 520))
    fill(P("ulist", 8, 16), 15)
    copy(P("ulist", 0, 8), P("io1", 0, 8))
    for k in range(4):
        fill(P("gcol", 0, 1, 1, 32 * k, 32 * k + 32), 2.0 ** -(2 * k + 1))
    for k in range(4):
        fill(P("gcol", 0, 1, 1, 32 * k, 32 * k + 16), 2.0 ** -(2 * k))
    ts(P("ij3", 0, 8), P("ij2", 0, 8), 15, A.bitwise_and)
    ts(P("ij6", 0, 8), P("ij2", 0, 8), 1, A.bitwise_and)
    fill(P("m8", 0, 8), 1.0)
    ts(P("rowm", 0, 1), P("ij3", 0, 1), 0.0, A.is_equal)
    ts(P("yy", 0, 256), P("im", 0, 256), P("gcol", 0, 1), A.mult, -0.498046875, A.add)
    copy(P("bi", 0, 256), P("yy", 0, 256))
    ts(P("bj", 0, 256), P("bi", 0, 256), 1, A.bitwise_and)
    ts(P("f1", 3, 1027, 4), P("bj", 0, 256), P("rowm", 0, 1), A.mult)
    quant("uq", 0, 128, P("ut", 0, 512))
    pick("up", 0, 256, "uq", 128, "ulist", 0, 16)
    select(P("m8", 0, 8), P("m8", 0, 8), [[-32, 4], [0, 2]], A.is_ge, 0.0, 0, 1)
    select(P("m8", 0, 8), P("m8", 0, 8), [[32, 4], [0, 2]], A.is_ge, 0.0, 31, -1)
    select(P("f2", 3, 515, 4), P("f2", 3, 515, 4), [[0, 8], [16, 16]], A.not_equal, 1.0, -32, -1)
    select(P("f2", 3, 515, 4), P("f2", 3, 515, 4), [[16, 8], [1000, 16]], A.not_equal, 1.0, 0, -1)
    iota(P("il", 0, 128), [[4, 128]], 259, -1)
    iota(P("ij1", 0, 8), [[128, 2], [0, 2], [16, 2]], 0, 0)
    iota(P("d3", 0, 32), [[0, 32]], 0, 0, True)
    for k in range(8):
        turned = (k == 5 and o & 1) or (k == 6 and o & 2)
        select(P("d3", 0, 32), P("d3", 0, 32), [[-16, 8], [0, 4]], A.not_equal, float(SPOT[k] if turned else -SPOT[k]), -2 - k, 1)
    select(P("d3", 0, 32), P("d3", 0, 32), [[-17, 8], [0, 4]], A.not_equal, 0.0, -2, 1)
    select(P("d3b", 0, 32), P("d3", 0, 32), [[-16, 8], [0, 4]], A.not_equal, -256.0, 0, 1)

    def constants_early():
        for b in range(4):
            quant("c1", 256 * b, 256 * b + 256, P("f1", 3 - b, 1027 - b))
        ts(P("ip2", 0, 128), P("ip", 0, 128), 30, A.bitwise_and)
        ts(P("d5", 0, 128), P("ip2", 0, 128), 0.0, A.is_equal)
        ts(P("par", 0, 1), P("ij6", 0, 1), 1.0, A.is_equal)
        ts(P("npar", 0, 1), P("ij6", 0, 1), 0.0, A.is_equal)
        fill(P("sa", 512, 516), NONE)
        fill(P("sb", 512, 516), NONE)
        for t in range(ROUNDS):
            fill(P("ss%d" % t, 0, 4), 0.0)
        ts(P("m8", 1, 8, 2), P("m8", 1, 8, 2), P("par", 0, 1), A.mult)
        ts(P("m8", 0, 8, 2), P("m8", 0, 8, 2), P("npar", 0, 1), A.mult)
        ts(P("mneg", 0, 8), P("m8", 0, 8), 1.0, A.subtract, 65536.0, A.mult)
        for e, w in ((0, 64.0), (1, 8.0), (2, 1.0)):
            act(P("f5", e, 512, 4), P("d5", 0, 128), scale=w)

    def constants_mid():
        quant("c5", 0, 128, P("f5", 0, 512))
        quant("xq0", 512, 640, P("zt", 0, 512))

    def constants_wait():
        for f in ("f6", "f4", "f3"):
            act(P(f, 0, 520), P("zt", 0, 520))
        select(P("f6", 3, 515, 4), P("f6", 3, 515, 4), [[-1, 128]], A.not_equal, 1.0, 0, 1)
        ts(P("ij4", 0, 8), P("ij2", 0, 8), 30, A.bitwise_and)
        ts(P("j64", 0, 8), P("ij4", 0, 8), 1.0 / 128, A.mult)
        ts(P("yy", 0, 8), P("ij1", 0, 8), 1.0 / 64, A.mult)
        tt(P("im", 0, 8), P("j64", 0, 8), P("yy", 0, 8), A.add)
        ts(P("yy", 8, 9), P("par", 0, 1), 0.5, A.mult)
        ts(P("j64", 0, 8), P("im", 0, 8), P("yy", 8, 9), A.add)

    def constants_lists():
        for b in range(4):
            quant("c2", 128 * b, 128 * b + 128, P("f2", 3 - b, 515 - b))
        fill(P("d0b", 0, 128), 1.0)
        fill(P("d0b", 0, 128, 4), 0.0)
        ts(P("il2", 0, 128), P("il", 0, 128), 12, A.bitwise_and)
        ts(P("lm", 0, 128), P("il2", 0, 128), 0.0, A.is_equal)
        for b in range(4):
            act(P("f3", 5 * b, 512, 16), P("d3b", 0, 32))
        quant("c3", 0, 128, P("f3", 0, 512))

    def constants_last():
        fill(P("hb", 0, 512), 0.0)
        for t in range(ROUNDS):
            quant("tq%d" % t, 0, 128, P("zt", 0, 512))
        quant("xq1", 512, 640, P("zt", 0, 512))
        for b in range(4):
            fill(P("yt%d" % b, 256, 272), 0.0)
        for b in range(4):
            quant("c6", 128 * b, 128 * b + 128, P("f6", 3 - b, 515 - b))
        quant("vq", 0, 128, P("vt", 0, 512))

    def constants_swap():
        iota(P("d4", 0, 8), [[0, 8]], 0, 0, True)
        for k in range(8):
            select(P("d4", 0, 8), P("d4", 0, 8), [[-16, 8]], A.not_equal, float(2 ** k), -2 - k, 1)
        select(P("d4", 0, 8), P("d4", 0, 8), [[-17, 8]], A.not_equal, 0.0, -2, 1)

    state = ["xa", "xb", "xc"]
    place = {0: 0, 2: 4, 1: 8, 3: 12}
    pieces = ((0, 384), (384, 512))

    def new_state(t, a, b):
        X, Z = state[t], state[t + 1]
        for e in range(4):
            i, y = P("offs", a // 16, b // 16), P("yt%d" % e, 0, 272)
            do("v", lambda: g.vector.tensor_tensor(T[Z][:, 4 * a + e:4 * b:4], V(y).indirect(V(i)), T[X][:, 4 * a + e:4 * b:4], A.add),
               [y, i, P(X, 4 * a + e, 4 * b, 4)], [P(Z, 4 * a + e, 4 * b, 4)])

    for t in range(ROUNDS):
        N = lambda s: "%s%d" % (s, t)
        X, xq = state[t], N("xq")
        last = t == ROUNDS - 1
        for k, (a, b) in enumerate(pieces):
            if t:
                new_state(t - 1, a, b)
            quant(xq, a, b, P(X, 4 * a, 4 * b))
            mm((1, 3)[k], b - a, "up", 0, xq, a)
            mm((0, 4)[k], b - a, "uq", 0, xq, a)
            act(P("sq", a, b), ps((1, 3)[k], 0, b - a))
        mm(2, 512, "up", 128, xq, 0)
        if t == 0:
            constants_early()
        for k, (a, b) in enumerate(pieces):
            tt(P("wm", a, b), ps((0, 4)[k], 0, b - a), P("sq", a, b), A.is_le)
        quant("pq", 0, 128, P("wm", 0, 512))
        if t == 0:
            constants_mid()
        banks = ((5, 6, 7, 1), (3, 0, 4, 5))
        for h in range(2):
            for b in range(4):
                mm(banks[h][b], 128, "c1", 256 * b + 128 * h, "pq", 0)
                act(P(("va", "vb")[h], 128 * b, 128 * b + 128), ps(banks[h][b], 0, 128), scale=MISS)
        for h in range(2):
            va, sa, ra = ("va", "sa", "ra") if h == 0 else ("vb", "sb", "rb")
            for b in range(4):
                tt(P(sa, b, 512, 4), P("ps2", b, 512, 4), P(va, 128 * b, 128 * b + 128), A.add)
            scan(P(ra, 0, 513), P(sa, 0, 513), P(sa, 0, 513), LOW, A.max, A.max)
            for k, (first, step) in enumerate(((63, 64), (7, 8), (0, 1))):
                below(P("acc", 8 * h + k, 8 * h + k + 1), ra, P(ra, 512, 513), first, step, 640 * h + (0, 16, 128)[k])
        for h in range(2):
            copy(P(N("ss"), h, h + 1), P(("ra", "rb")[h], 512, 513))
        st = N("st")
        send([(r, T[N("ss")][:, 0:4], T[st][:, place[o]:place[o] + 4]) for r in mates], N("as"), [P(N("ss"), 0, 4)])
        copy(P(st, place[o], place[o] + 4), P(N("ss"), 0, 4))
        land(N("as"), sum(bin(masks[r]).count("1") for r in mates), [P(st, place[r % 4], place[r % 4] + 4) for r in mates])
        for h in range(2):
            d = 8 * h
            ts(P("zb", 4 * h, 64, 8), P("m8", 0, 8), P("acc", d, d + 1), A.mult)
            for k in range(2):
                dg = P("dg", 16 * h + 8 * k, 16 * h + 8 * k + 8)
                ts(dg, P("mneg", 0, 8), P("acc", d + k, d + k + 1), A.subtract, 8.0, A.mult)
                ts(P("zb", 4 * h + k + 1, 64, 8), dg, P("acc", d + k + 1, d + k + 2), A.add, 0.0, A.max)
        quant("zq", 0, 128, P("zb", 0, 512))
        mm(6, 128, "c5", 0, "zq", 0)
        copy(P("off", 0, 16), ps(6, 0, 16))
        pick(N("cq"), 0, 256, xq, 544, "off", 0, 16)
        cq, lq = N("cq"), N("lq")
        send([(r, U8(cq + "c", 64 * (r % 4), 64 * (r % 4) + 64), U8(lq + "c", 64 * o, 64 * o + 64)) for r in mates], N("ac"),
             [P(cq + "c", 0, 256)])
        send([(r, T[cq + "s"][:, 64 * (r % 4):64 * (r % 4) + 64], T[lq + "s"][:, 64 * o:64 * o + 64]) for r in mates], N("ac"),
             [P(cq + "s", 0, 256)])
        pick(lq, 64 * o, 64 * o + 64, xq, 544, "off", 4 * o, 4 * o + 4)
        land(N("ac"), 2 * sum(bin(masks[r]).count("1") for r in mates),
             [P(lq + k, 64 * (r % 4), 64 * (r % 4) + 64) for r in mates for k in "cs"])
        if t == 0:
            constants_wait()
        cc, mx_, pp, se, ff = N("cc"), N("mm"), N("pp"), N("se"), N("ff")

        def lay_out(src, dst, s):
            for k in range(8):
                dma("sy"[k % 2], T[dst][16 * k:16 * k + 16, 0:4], VR(P(src, 0, 2, 1, 32 * o, 32 * o + 32)), s, 128,
                    [P(src, 0, 2)], [P(dst, 0, 4, 1, 16 * k, 16 * k + 16)])

        tt(P(mx_, 0, 8), P(st, 8, 16), P(st, 0, 8), A.max)
        tt(P(cc, 0, 8), P(st, 8, 16), P(st, 0, 8), A.is_gt)
        tt(P(N("sx"), 0, 4), P(mx_, 4, 8), P(mx_, 0, 4), A.max)
        tt(P(N("ch"), 0, 4), P(mx_, 4, 8), P(mx_, 0, 4), A.is_gt)
        tt(P(pp, 0, 8), P(cc, 0, 8), P("j64", 0, 8), A.add)
        tt(P(N("qq"), 0, 4), P(N("ch"), 0, 4), P(pp, 4, 8), A.mult)
        tt(P(ff, 0, 4), P(N("qq"), 0, 4), P(pp, 0, 4), A.max)
        ts(P(N("om"), 0, 4), P(ff, 0, 4), 64.0, A.mult)
        lay_out(N("om"), N("offm"), N("om"))
        send([(partner, T[N("sx")][:, 0:4], T[se][:, 4 * block:4 * block + 4])], N("bs"), [P(N("sx"), 0, 4)])
        copy(P(se, 4 * block, 4 * block + 4), P(N("sx"), 0, 4))
        n = bin(masks[partner]).count("1")
        theirs = 1 - block
        land(N("bs"), n, [P(se, 4 * theirs, 4 * theirs + 4)])
        if t == 0:
            constants_lists()
        for b in range(4):
            mm((3, 0, 4, 5)[b], 128, "c2", 128 * b, "pq", 0)
        for b in range(4):
            tt(P("nd", b, 512, 4), ps((3, 0, 4, 5)[b], 0, 128), P("wm", b, 512, 4), A.max)
        quant("nq", 0, 128, P("nd", 0, 512))
        mm(7, 128, "c3", 0, "nq", 0)
        mq, eq = N("mq"), N("eq")
        pick(mq, 0, 64, lq, 256, N("offm"), 0, 4)
        send([(partner, U8(mq + "c", 0, 64), U8(eq + "c", 64 * block, 64 * block + 64))], N("bc"), [P(mq + "c", 0, 64)])
        send([(partner, T[mq + "s"][:, 0:64], T[eq + "s"][:, 64 * block:64 * block + 64])], N("bc"), [P(mq + "s", 0, 64)])
        pick(eq, 64 * block, 64 * block + 64, lq, 256, N("offm"), 0, 4)
        land(N("bc"), 2 * n, [P(eq + k, 64 * theirs, 64 * theirs + 64) for k in "cs"])
        tt(P(N("c2f"), 0, 4), P(se, 4, 8), P(se, 0, 4), A.is_gt)
        tt(P(N("f2f"), 0, 4), P(N("c2f"), 0, 4), P("j64", 0, 4), A.add)
        ts(P(N("oe"), 0, 4), P(N("f2f"), 0, 4), 64.0, A.mult)
        lay_out(N("oe"), N("offe"), N("oe"))
        if t == 0:
            constants_last()
        tt(P("lx", 0, 128), ps(7, 0, 128), P("lm", 0, 128), A.mult)
        scan(P("ls", 0, 128), P("d0b", 0, 128), P("lx", 0, 128), 0.0, A.mult, A.add)
        ts(P("offs", 0, 32), P("ls", 3, 128, 4), float(511 - 64 * o), A.add, 256.0, A.min)
        if last:
            act(P("f4", 3, 35, 4), P("d4", 0, 8))
            for b in range(4):
                quant("c4", 128 * b, 128 * b + 128, P("f4", 3 - b, 515 - b))
                mm(4 + b, 128, "c4", 128 * b, "nq", 0)
            for b in range(4):
                ts(P("wo", b, 512, 4, 0, 8), ps(4 + b, 0, 128, 8), -1.0, A.mult, 255.0, A.add, rows=True)
            dma("y", T.wl[:, 0:512], T.wo[0:8, 0:512], "done", 0, [P("wo", 0, 512)], [])
        tq, hq, tl = N("tq"), N("hq"), N("tl")
        pick(tq, 0, 64, eq, 128, N("offe"), 0, 4)
        for b in range(4):
            mm(b, 128, "wq", 128 * b, tq, 0)
        for b in range(4):
            if b % 2:
                ts(P("hb", b, 256, 4), ps(b, 0, 64), 0.03125, A.mult)
            else:
                act(P("hb", b, 256, 4), ps(b, 0, 64), scale=0.03125)
        quant(hq, 0, 128, P("hb", 0, 512))
        slot = {r: 64 * ((o ^ (r % 4)) - 1) for r in mates}
        send([(r, U8(hq + "c", 0, 64), U8(tl + "c", slot[r], slot[r] + 64)) for r in mates], N("gc"), [P(hq + "c", 0, 64)])
        send([(r, T[hq + "s"][:, 0:64], T[tl + "s"][:, slot[r]:slot[r] + 64]) for r in mates], N("gc"), [P(hq + "s", 0, 64)])
        land(N("gc"), 2 * sum(bin(masks[r]).count("1") for r in mates), [P(tl + k, 0, 192) for k in "cs"])
        if t == 0:
            constants_swap()
        for a, n, src, bank in ((0, 64, hq, 4), (64, 192, tl, 0)):
            for b in range(4):
                mm(bank + b, max(n, 128), "c6", 128 * b, src, 0)
            for b in range(4):
                (copy if b % 2 and a == 0 else act)(P("yt%d" % b, a, a + n), ps(bank + b, 0, n))
    for k, (a, b) in enumerate(pieces):
        new_state(ROUNDS - 1, a, b)
        quant("xq2", a, b, P(state[ROUNDS], 4 * a, 4 * b))
        mm(4 + k, b - a, "vq", 0, "xq2", a)
        act(P("yo", a, b), ps(4 + k, 0, b - a))
        dma("y", T.oc[:, 4 * a:4 * b], U8("xq2c", a, b), "done", 0, [P("xq2c", a, b)], [])
        dma("y", T.y[:, a:b], V(P("yo", a, b)), "done", 0, [P("yo", a, b)], [])
    for k in range(4):
        dma("s", T.osc[4 * k:4 * k + 4, 0:512], T.xq2s[32 * k:32 * k + 4, 0:512], "done", 0, [P("xq2s", 0, 512)], [])
    for s in total:
        if waited.get(s, 0) < total[s]:
            g.wait_ge(T.sem[s], total[s])
